import numpy as np
import ml_dtypes


def mxq(x, axis, fmt="e4m3"):
    dtype, down = {"e4m3": (ml_dtypes.float8_e4m3fn, 7), "e5m2": (ml_dtypes.float8_e5m2, 14)}[fmt]
    v = np.moveaxis(np.asarray(x, np.float32).astype(ml_dtypes.bfloat16).astype(np.float64), axis, -1)
    blocks = v.reshape(v.shape[:-1] + (-1, 32))
    amax = np.abs(blocks).max(-1, keepdims=True)
    byte = np.maximum(np.where(amax > 0, np.frexp(amax)[1] - 1 + 127, 0) - down, 1)
    scale = np.exp2(byte - 127.0)
    codes = (blocks / scale).astype(np.float32).astype(dtype).astype(np.float64)
    return np.moveaxis((codes * scale).reshape(v.shape), -1, axis)


WIDE = False


def mx_kscale(k):
    if not WIDE:
        return np.ones(k)
    levels = np.array([10, -10, 5, -5, 0])
    if k % 512:
        return np.exp2(np.random.permutation(np.resize(levels, k // 32))).repeat(32)
    a = np.empty((k // 512, 16))
    for p in range(k // 512):
        a[p, :8] = np.random.permutation(np.resize(levels, 8))
        for g in range(8):
            far = levels[np.abs(levels - a[p, g]) >= 10]
            a[p, g + 8] = far[np.random.randint(len(far))]
    return np.exp2(a.ravel()).repeat(32)


def f64(x):
    return np.asarray(x).astype(np.float64)


def striped8(idx):
    return np.asarray(idx).reshape(8, -1, 16).transpose(0, 2, 1).reshape(128, -1).astype(np.uint16)


def unstriped8(offs):
    return offs.reshape(8, 16, -1).transpose(0, 2, 1).reshape(8, -1).astype(np.int64)


def pick8(x, idx, run):
    r = np.arange(len(x))
    return x[r[:, None], idx[r % (8 * run) // run]]


E2M1 = np.array([0.0, 0.5, 1.0, 1.5, 2.0, 3.0, 4.0, 6.0, -0.0, -0.5, -1.0, -1.5, -2.0, -3.0, -4.0, -6.0])


def pack_weight(w, fmt):
    k, n = w.shape
    w = f64(np.asarray(w, np.float32).astype(ml_dtypes.bfloat16)).reshape(k // 32, 32, n)
    amax = np.abs(w).max(1)
    if fmt == "e4m3":
        byte = np.frexp(amax)[1] - 1 + 127 - 7
    else:
        mant, ex = np.frexp(amax / 6.0)
        byte = np.where(mant > 0.5, ex, ex - 1) + 127
    byte = np.clip(np.where(amax > 0, byte, 1), 1, 254)
    scaled = (w * np.exp2(127.0 - byte)[:, None, :]).reshape(k, n).astype(np.float32)
    by_word = np.ascontiguousarray(scaled.reshape(k // 512, 128, 4, n).transpose(0, 1, 3, 2))
    if fmt == "e4m3":
        words = by_word.astype(ml_dtypes.float8_e4m3fn).view(np.uint8)
    else:
        c = by_word.astype(ml_dtypes.float4_e2m1fn).view(np.uint8) & 0xF
        words = (c[..., 0::2] | (c[..., 1::2] << 4)).reshape(k // 512, 128, 2 * n)
    return np.ascontiguousarray(words), np.ascontiguousarray(byte.astype(np.uint8).reshape(k // 512, 16, n))


def unpack_weight(words, scales, fmt):
    g, _, n = scales.shape
    words = np.ascontiguousarray(words).reshape(g, 128, n, -1)
    if fmt == "e4m3":
        vals = words.view(ml_dtypes.float8_e4m3fn).astype(np.float64)
    else:
        nib = np.empty((g, 128, n, 4), np.uint8)
        nib[..., 0::2] = words & 0xF
        nib[..., 1::2] = words >> 4
        vals = E2M1[nib]
    vals = vals * np.repeat(np.exp2(scales.astype(np.float64) - 127.0), 8, axis=1)[..., None]
    return vals.transpose(0, 1, 3, 2).reshape(g * 512, n)


def sigmoid(v):
    return 1.0 / (1.0 + np.exp(-v))


def bf(x):
    return np.asarray(x, np.float32).astype(ml_dtypes.bfloat16)


def planes(Y):
    r, m = Y.shape
    b = f64(bf(Y)).reshape(r // 32, 32, m)
    amax = np.abs(b).max(1)
    byte = np.clip(np.where(amax > 0, np.frexp(amax)[1] - 1 + 127 - 7, 1), 1, 254)
    codes = (b * np.exp2(127.0 - byte)[:, None, :]).reshape(r, m).astype(np.float32).astype(ml_dtypes.float8_e4m3fn).view(np.uint8)
    words = codes.reshape(r // 512, 128, 4, m).transpose(0, 1, 3, 2)
    return np.ascontiguousarray(words), np.ascontiguousarray(byte.astype(np.uint8).reshape(r // 512, 16, m))


K, T, J, N, L = 512, 512, 512, 512, 512


def setup_inputs():
    n = np.random.standard_normal
    idx = np.stack([np.random.randint(0, T, J) for _ in range(8)])
    idx2 = np.stack([np.random.randint(0, T, J) for _ in range(8)])
    fk = mx_kscale(K)
    fl = mx_kscale(L)
    xtp = pack_weight(n((K, T)) / fk[:, None], "e2m1")
    wp = pack_weight(n((K, N)) * 1 / np.sqrt(K) * fk[:, None], "e4m3")
    wqp = pack_weight(n((L, N)) * 1 / np.sqrt(L) * fl[:, None], "e4m3")
    return {
        "xt_words": xtp[0],
        "xt_scales": xtp[1],
        "w_words": wp[0],
        "w_scales": wp[1],
        "qx": (n((L, J)) / fl[:, None]).astype(np.float32),
        "wq_words": wqp[0],
        "wq_scales": wqp[1],
        "offs": striped8(idx),
        "offs2": striped8(idx2),
    }


def reference(xt_words, xt_scales, w_words, w_scales, qx, wq_words, wq_scales, offs, offs2):
    idx = unstriped8(offs)
    idx2 = unstriped8(offs2)
    xtu = unpack_weight(xt_words, xt_scales, "e2m1")
    wu = unpack_weight(w_words, w_scales, "e4m3")
    wqu = unpack_weight(wq_words, wq_scales, "e4m3")
    z = wu.T @ xtu
    qxq = mxq(f64(qx), 0, "e4m3")
    g = wqu.T @ qxq
    y = pick8(z, idx2, 64) + sigmoid(g) * (pick8(z, idx, 64) - pick8(z, idx2, 64))
    words, scales = planes(y)
    return y, words, scales

@@ -1,0 +1,239 @@
+from contextlib import ExitStack
+
+import concourse.mybir as mybir
+
+F32 = mybir.dt.float32
+BF16 = mybir.dt.bfloat16
+I32 = mybir.dt.int32
+U16 = mybir.dt.uint16
+U8 = mybir.dt.uint8
+FP8X4 = mybir.dt.float8_e4m3fn_x4
+FP4X4 = mybir.dt.float4_e2m1fn_x4
+MULT = mybir.AluOpType.mult
+ADD = mybir.AluOpType.add
+SIGMOID = mybir.ActivationFunctionType.Sigmoid
+
+P = 128
+PACK = 4
+W = 512
+BANK = 512
+FLOPS = 2 * 2 * 512 * 512 * 512
+
+CHUNKS = ((0, 256), (256, 128), (384, 128))
+QX_LOADS = ((0, 256), (256, 256))
+
+
+def load_scales(queue, plane, scales, quadrants):
+    for q in quadrants:
+        queue.dma_start(
+            out=plane[32 * q : 32 * q + 4, :].bitcast(I32),
+            in_=scales[0, 4 * q : 4 * q + 4, :].bitcast(I32),
+        )
+
+
+def deal_words(nc, dealt, raw):
+    nc.vector.tensor_copy(
+        out=dealt[:].rearrange("p (t c i) -> p c t i", t=PACK, i=4),
+        in_=raw[:].rearrange("p (c i t) -> p c t i", t=PACK, i=4),
+    )
+
+
+def deal_scales(nc, dealt, raw):
+    nc.vector.tensor_copy(
+        out=dealt[:].rearrange("p (t c i) -> p c t i", t=PACK, i=16),
+        in_=raw[:].rearrange("p (c i t) -> p c t i", t=PACK, i=16),
+    )
+
+
+def interleave_views(grouped, rows):
+    return (
+        grouped.rearrange("p (c i t) -> p c t i", t=PACK, i=4),
+        rows.rearrange("p t (c i) -> p c t i", i=4),
+    )
+
+
+def tile_list_head_blend_two_lists_pl_kernel(
+    tc, xt_words, xt_scales, w_words, w_scales, qx, wq_words, wq_scales, offs, offs2, out_0, out_1, out_2
+):
+    nc = tc.nc
+    with ExitStack() as ctx:
+        keep = ctx.enter_context(tc.tile_pool(name="keep", bufs=1))
+        psum = ctx.enter_context(tc.psum_pool(name="psum", bufs=1))
+
+        list_a = keep.tile([P, W // 16], U16, name="list_a")
+        list_b = keep.tile([P, W // 16], U16, name="list_b")
+        wq_raw = keep.tile([P, W], I32, name="wq_raw")
+        w_raw = keep.tile([P, W], I32, name="w_raw")
+        x_codes = keep.tile([P, 2 * W], U8, name="x_codes", align_bytes=64)
+        wq_plane_raw = keep.tile([P, W], U8, name="wq_plane_raw")
+        w_plane_raw = keep.tile([P, W], U8, name="w_plane_raw")
+        x_plane = keep.tile([P, W], U8, name="x_plane", align_bytes=64)
+        q_rows = [keep.tile([P, PACK, n], F32, name="q_rows%d" % i) for i, (j0, n) in enumerate(QX_LOADS)]
+
+        nc.vector.memset(wq_plane_raw[:].bitcast(I32), 0)
+        nc.vector.memset(w_plane_raw[:].bitcast(I32), 0)
+        nc.vector.memset(x_plane[:].bitcast(I32), 0)
+
+        qx_rows = qx.rearrange("(p r) j -> p r j", r=PACK)
+        nc.sync.dma_start(out=wq_raw[:], in_=wq_words[0].rearrange("p n t -> p (n t)").bitcast(I32))
+        load_scales(nc.sync, wq_plane_raw, wq_scales, (0, 1, 2, 3))
+        load_scales(nc.sync, w_plane_raw, w_scales, (0, 1))
+        nc.sync.dma_start(out=q_rows[0][:], in_=qx_rows[:, :, 0:256])
+        load_scales(nc.sync, w_plane_raw, w_scales, (2, 3))
+        nc.sync.dma_start(out=w_raw[:], in_=w_words[0].rearrange("p n t -> p (n t)").bitcast(I32))
+        nc.sync.dma_start(out=x_codes[:].bitcast(I32), in_=xt_words[0].bitcast(I32))
+        load_scales(nc.sync, x_plane, xt_scales, (0, 1, 2, 3))
+        nc.sync.dma_start(list_a[:], offs)
+        nc.sync.dma_start(list_b[:], offs2)
+        nc.sync.dma_start(out=q_rows[1][:], in_=qx_rows[:, :, 256:512])
+
+        wq_codes = keep.tile([P, W], I32, name="wq_codes", align_bytes=64)
+        w_codes = keep.tile([P, W], I32, name="w_codes", align_bytes=64)
+        wq_plane = keep.tile([P, W], U8, name="wq_plane", align_bytes=64)
+        w_plane = keep.tile([P, W], U8, name="w_plane", align_bytes=64)
+        deal_words(nc, wq_codes, wq_raw)
+        deal_scales(nc, wq_plane, wq_plane_raw)
+
+        q_codes = [keep.tile([P, n], I32, name="q_codes%d" % c, align_bytes=64) for c, (j0, n) in enumerate(CHUNKS)]
+        q_plane = [keep.tile([P, n], U8, name="q_plane%d" % c, align_bytes=64) for c, (j0, n) in enumerate(CHUNKS)]
+        q_bf = [
+            keep.tile([P, PACK * n], BF16, name="q_bf%d" % c, tag="stage%d" % c, align_bytes=64)
+            for c, (j0, n) in enumerate(CHUNKS)
+        ]
+
+        def round_q(c, on_vector):
+            j0, n = CHUNKS[c]
+            i = j0 // 256
+            lo = j0 - QX_LOADS[i][0]
+            dst, src = interleave_views(q_bf[c][:], q_rows[i][:, :, lo : lo + n])
+            if on_vector:
+                nc.vector.tensor_copy(out=dst, in_=src)
+            else:
+                nc.scalar.copy(out=dst, in_=src)
+
+        def quantise_q(c):
+            nc.vector.quantize_mx(out=q_codes[c][:].bitcast(FP8X4), scales=q_plane[c][:], in_=q_bf[c][:])
+
+        gate_a = [keep.tile([P, PACK, n], F32, name="gate_a%d" % c) for c, (j0, n) in enumerate(CHUNKS)]
+        gate_b = [keep.tile([P, PACK, n], F32, name="gate_b%d" % c) for c, (j0, n) in enumerate(CHUNKS)]
+
+        def gates(c, t0, t1, bank):
+            j0, n = CHUNKS[c]
+            g = psum.tile([P, t1 - t0, n], F32, name="g%d_%d" % (c, t0), tag="bank%d" % bank)
+            for t in range(t0, t1):
+                nc.tensor.matmul_mx(
+                    out=g[:, t - t0, :],
+                    lhsT=wq_codes[:, t * P : (t + 1) * P].bitcast(FP8X4),
+                    lhsT_scale=wq_plane[:, t * P : (t + 1) * P],
+                    rhs=q_codes[c][:].bitcast(FP8X4),
+                    rhs_scale=q_plane[c][:],
+                    start=True,
+                    stop=True,
+                )
+            nc.scalar.activation(out=gate_a[c][:, t0:t1, :], in_=g[:], func=SIGMOID)
+            nc.scalar.activation(out=gate_b[c][:, t0:t1, :], in_=g[:], func=SIGMOID, scale=-1.0)
+
+        round_q(0, True)
+        quantise_q(0)
+        deal_words(nc, w_codes, w_raw)
+        deal_scales(nc, w_plane, w_plane_raw)
+
+        z = [keep.tile([P, W], F32, name="z%d" % t) for t in range(PACK)]
+
+        def features(t, lo, hi, bank, on_vector):
+            acc = psum.tile([P, hi - lo], F32, name="z_acc%d_%d" % (t, lo), tag="bank%d" % bank)
+            nc.tensor.matmul_mx(
+                out=acc[:],
+                lhsT=w_codes[:, t * P : (t + 1) * P].bitcast(FP8X4),
+                lhsT_scale=w_plane[:, t * P : (t + 1) * P],
+                rhs=x_codes[:, 2 * lo : 2 * hi].bitcast(FP4X4),
+                rhs_scale=x_plane[:, lo:hi],
+                start=True,
+                stop=True,
+            )
+            if on_vector:
+                nc.vector.tensor_copy(out=z[t][:, lo:hi], in_=acc[:])
+            else:
+                nc.scalar.copy(out=z[t][:, lo:hi], in_=acc[:])
+
+        gates(0, 0, 2, 4)
+        features(0, 0, 256, 0, True)
+        features(0, 256, 512, 7, True)
+        features(1, 0, 512, 1, False)
+        gates(0, 2, 4, 0)
+        features(2, 0, 512, 7, False)
+        features(3, 0, 512, 1, False)
+
+        y_codes = keep.tile([P, W], I32, name="y_codes", align_bytes=64)
+        y_plane = keep.tile([P, W], U8, name="y_plane", align_bytes=64)
+        out_rows = out_0.rearrange("(p t) j -> p t j", t=PACK)
+        out_words = out_1[0].rearrange("p n t -> p (n t)")
+        part_a = [keep.tile([P, PACK, n], F32, name="part_a%d" % c) for c, (j0, n) in enumerate(CHUNKS)]
+        part_b = [keep.tile([P, PACK, n], F32, name="part_b%d" % c) for c, (j0, n) in enumerate(CHUNKS)]
+        y_bf = [keep.tile([P, PACK * n], BF16, name="y_bf%d" % c, align_bytes=64) for c, (j0, n) in enumerate(CHUNKS)]
+        y = {}
+
+        def look_up(c, t):
+            j0, n = CHUNKS[c]
+            cols = slice(j0 // 16, (j0 + n) // 16)
+            nc.vector.tensor_tensor(part_a[c][:, t, :], z[t][:].indirect(list_a[:, cols]), gate_a[c][:, t, :], MULT)
+            nc.vector.tensor_tensor(part_b[c][:, t, :], z[t][:].indirect(list_b[:, cols]), gate_b[c][:, t, :], MULT)
+
+        def add(c, t0, t1):
+            nc.vector.tensor_tensor(y[c][:, t0:t1, :], part_a[c][:, t0:t1, :], part_b[c][:, t0:t1, :], ADD)
+
+        def store(c):
+            j0, n = CHUNKS[c]
+            nc.sync.dma_start(out=out_rows[:, :, j0 : j0 + n], in_=y[c][:])
+
+        def round_y(c, on_vector):
+            dst, src = interleave_views(y_bf[c][:], y[c][:])
+            if on_vector:
+                nc.vector.tensor_copy(out=dst, in_=src)
+            else:
+                nc.scalar.copy(out=dst, in_=src)
+
+        def planes(c):
+            j0, n = CHUNKS[c]
+            nc.vector.quantize_mx(
+                out=y_codes[:, j0 : j0 + n].bitcast(FP8X4), scales=y_plane[:, j0 : j0 + n], in_=y_bf[c][:]
+            )
+            nc.sync.dma_start(out=out_words[:, 4 * j0 : 4 * (j0 + n)].bitcast(I32), in_=y_codes[:, j0 : j0 + n])
+
+        round_q(1, False)
+        round_q(2, False)
+        for t in range(PACK):
+            look_up(0, t)
+        quantise_q(1)
+        gates(1, 0, 4, 5)
+        y[0] = keep.tile([P, PACK, CHUNKS[0][1]], F32, name="y0", tag="stage1", align_bytes=64)
+        add(0, 0, 4)
+        store(0)
+        quantise_q(2)
+        gates(2, 0, 4, 6)
+        round_y(0, False)
+        for t in range(PACK):
+            look_up(1, t)
+        y[1] = keep.tile([P, PACK, CHUNKS[1][1]], F32, name="y1", tag="stage2", align_bytes=64)
+        look_up(2, 0)
+        add(1, 0, 4)
+        store(1)
+        round_y(1, False)
+        y[2] = keep.tile([P, PACK, CHUNKS[2][1]], F32, name="y2")
+        look_up(2, 1)
+        look_up(2, 2)
+        add(2, 0, 2)
+        look_up(2, 3)
+        add(2, 2, 3)
+        planes(0)
+        add(2, 3, 4)
+        store(2)
+        planes(1)
+        round_y(2, True)
+        planes(2)
+        for q in range(4):
+            queue = nc.scalar if q % 2 else nc.sync
+            queue.dma_start(
+                out=out_2[0, 4 * q : 4 * q + 4, :].bitcast(I32),
+                in_=y_plane[32 * q : 32 * q + 4, :].bitcast(I32),
+            )

@@ -19,14 +19,13 @@ W = 512
 BANK = 512
 FLOPS = 2 * 2 * 512 * 512 * 512
 
-CHUNKS = ((0, 256), (256, 128), (384, 128))
-QX_LOADS = ((0, 256), (256, 256))
+HALF = 256
 
 
-def load_scales(queue, plane, scales, quadrants):
+def load_scales(queue, plane, first_row, scales, quadrants):
     for q in quadrants:
         queue.dma_start(
-            out=plane[32 * q : 32 * q + 4, :].bitcast(I32),
+            out=plane[32 * q + first_row : 32 * q + first_row + 4, :].bitcast(I32),
             in_=scales[0, 4 * q : 4 * q + 4, :].bitcast(I32),
         )
 
@@ -65,78 +64,69 @@ def tile_list_head_blend_two_lists_pl_kernel(
         wq_raw = keep.tile([P, W], I32, name="wq_raw")
         w_raw = keep.tile([P, W], I32, name="w_raw")
         x_codes = keep.tile([P, 2 * W], U8, name="x_codes", align_bytes=64)
-        wq_plane_raw = keep.tile([P, W], U8, name="wq_plane_raw")
-        w_plane_raw = keep.tile([P, W], U8, name="w_plane_raw")
+        planes_raw = keep.tile([P, W], U8, name="planes_raw")
         x_plane = keep.tile([P, W], U8, name="x_plane", align_bytes=64)
-        q_rows = [keep.tile([P, PACK, n], F32, name="q_rows%d" % i) for i, (j0, n) in enumerate(QX_LOADS)]
+        q_rows = [keep.tile([P, PACK, HALF], F32, name="q_rows%d" % h) for h in range(2)]
 
-        nc.vector.memset(wq_plane_raw[:].bitcast(I32), 0)
-        nc.vector.memset(w_plane_raw[:].bitcast(I32), 0)
+        nc.vector.memset(planes_raw[:].bitcast(I32), 0)
         nc.vector.memset(x_plane[:].bitcast(I32), 0)
 
         qx_rows = qx.rearrange("(p r) j -> p r j", r=PACK)
         nc.sync.dma_start(out=wq_raw[:], in_=wq_words[0].rearrange("p n t -> p (n t)").bitcast(I32))
-        load_scales(nc.sync, wq_plane_raw, wq_scales, (0, 1, 2, 3))
-        load_scales(nc.sync, w_plane_raw, w_scales, (0, 1))
-        nc.sync.dma_start(out=q_rows[0][:], in_=qx_rows[:, :, 0:256])
-        load_scales(nc.sync, w_plane_raw, w_scales, (2, 3))
+        load_scales(nc.scalar, planes_raw, 4, wq_scales, (0, 1, 2))
+        load_scales(nc.sync, planes_raw, 4, wq_scales, (3,))
+        load_scales(nc.sync, planes_raw, 0, w_scales, (0, 1))
+        nc.sync.dma_start(out=q_rows[0][:], in_=qx_rows[:, :, 0:HALF])
+        load_scales(nc.sync, planes_raw, 0, w_scales, (2, 3))
         nc.sync.dma_start(out=w_raw[:], in_=w_words[0].rearrange("p n t -> p (n t)").bitcast(I32))
         nc.sync.dma_start(out=x_codes[:].bitcast(I32), in_=xt_words[0].bitcast(I32))
-        load_scales(nc.sync, x_plane, xt_scales, (0, 1, 2, 3))
+        load_scales(nc.sync, x_plane, 0, xt_scales, (0, 1, 2, 3))
         nc.sync.dma_start(list_a[:], offs)
         nc.sync.dma_start(list_b[:], offs2)
-        nc.sync.dma_start(out=q_rows[1][:], in_=qx_rows[:, :, 256:512])
+        nc.sync.dma_start(out=q_rows[1][:], in_=qx_rows[:, :, HALF:W])
 
         wq_codes = keep.tile([P, W], I32, name="wq_codes", align_bytes=64)
-        w_codes = keep.tile([P, W], I32, name="w_codes", align_bytes=64)
-        wq_plane = keep.tile([P, W], U8, name="wq_plane", align_bytes=64)
-        w_plane = keep.tile([P, W], U8, name="w_plane", align_bytes=64)
+        planes_dealt = keep.tile([P, W], U8, name="planes_dealt", align_bytes=64)
         deal_words(nc, wq_codes, wq_raw)
-        deal_scales(nc, wq_plane, wq_plane_raw)
 
-        q_codes = [keep.tile([P, n], I32, name="q_codes%d" % c, align_bytes=64) for c, (j0, n) in enumerate(CHUNKS)]
-        q_plane = [keep.tile([P, n], U8, name="q_plane%d" % c, align_bytes=64) for c, (j0, n) in enumerate(CHUNKS)]
-        q_bf = [
-            keep.tile([P, PACK * n], BF16, name="q_bf%d" % c, tag="stage%d" % c, align_bytes=64)
-            for c, (j0, n) in enumerate(CHUNKS)
-        ]
+        q_codes = [keep.tile([P, HALF], I32, name="q_codes%d" % h, align_bytes=64) for h in range(2)]
+        q_plane = [keep.tile([P, HALF], U8, name="q_plane%d" % h, align_bytes=64) for h in range(2)]
+        q_bf = [keep.tile([P, PACK * HALF], BF16, name="q_bf%d" % h, tag="stage%d" % h, align_bytes=64) for h in range(2)]
 
-        def round_q(c, on_vector):
-            j0, n = CHUNKS[c]
-            i = j0 // 256
-            lo = j0 - QX_LOADS[i][0]
-            dst, src = interleave_views(q_bf[c][:], q_rows[i][:, :, lo : lo + n])
+        def round_rows(grouped, rows, on_vector):
+            dst, src = interleave_views(grouped, rows)
             if on_vector:
                 nc.vector.tensor_copy(out=dst, in_=src)
             else:
                 nc.scalar.copy(out=dst, in_=src)
 
-        def quantise_q(c):
-            nc.vector.quantize_mx(out=q_codes[c][:].bitcast(FP8X4), scales=q_plane[c][:], in_=q_bf[c][:])
+        def quantise_q(h):
+            nc.vector.quantize_mx(out=q_codes[h][:].bitcast(FP8X4), scales=q_plane[h][:], in_=q_bf[h][:])
 
-        gate_a = [keep.tile([P, PACK, n], F32, name="gate_a%d" % c) for c, (j0, n) in enumerate(CHUNKS)]
-        gate_b = [keep.tile([P, PACK, n], F32, name="gate_b%d" % c) for c, (j0, n) in enumerate(CHUNKS)]
+        gate_a = [keep.tile([P, PACK, HALF], F32, name="gate_a%d" % h) for h in range(2)]
+        gate_b = [keep.tile([P, PACK, HALF], F32, name="gate_b%d" % h) for h in range(2)]
 
-        def gates(c, t0, t1, bank):
-            j0, n = CHUNKS[c]
-            g = psum.tile([P, t1 - t0, n], F32, name="g%d_%d" % (c, t0), tag="bank%d" % bank)
+        def gates(h, t0, t1, bank):
+            g = psum.tile([P, t1 - t0, HALF], F32, name="g%d_%d" % (h, t0), tag="bank%d" % bank)
             for t in range(t0, t1):
                 nc.tensor.matmul_mx(
                     out=g[:, t - t0, :],
                     lhsT=wq_codes[:, t * P : (t + 1) * P].bitcast(FP8X4),
-                    lhsT_scale=wq_plane[:, t * P : (t + 1) * P],
-                    rhs=q_codes[c][:].bitcast(FP8X4),
-                    rhs_scale=q_plane[c][:],
+                    lhsT_scale=planes_dealt[4:P, t * P : (t + 1) * P],
+                    rhs=q_codes[h][:].bitcast(FP8X4),
+                    rhs_scale=q_plane[h][:],
                     start=True,
                     stop=True,
                 )
-            nc.scalar.activation(out=gate_a[c][:, t0:t1, :], in_=g[:], func=SIGMOID)
-            nc.scalar.activation(out=gate_b[c][:, t0:t1, :], in_=g[:], func=SIGMOID, scale=-1.0)
+            nc.scalar.activation(out=gate_a[h][:, t0:t1, :], in_=g[:], func=SIGMOID)
+            nc.scalar.activation(out=gate_b[h][:, t0:t1, :], in_=g[:], func=SIGMOID, scale=-1.0)
 
-        round_q(0, True)
+        round_rows(q_bf[0][:, : PACK * 160], q_rows[0][:, :, :160], True)
+        round_rows(q_bf[0][:, PACK * 160 :], q_rows[0][:, :, 160:], False)
         quantise_q(0)
+        deal_scales(nc, planes_dealt, planes_raw)
+        w_codes = keep.tile([P, W], I32, name="w_codes", tag="stage0", align_bytes=64)
         deal_words(nc, w_codes, w_raw)
-        deal_scales(nc, w_plane, w_plane_raw)
 
         z = [keep.tile([P, W], F32, name="z%d" % t) for t in range(PACK)]
 
@@ -145,7 +135,7 @@ def tile_list_head_blend_two_lists_pl_kernel(
             nc.tensor.matmul_mx(
                 out=acc[:],
                 lhsT=w_codes[:, t * P : (t + 1) * P].bitcast(FP8X4),
-                lhsT_scale=w_plane[:, t * P : (t + 1) * P],
+                lhsT_scale=planes_dealt[:, t * P : (t + 1) * P],
                 rhs=x_codes[:, 2 * lo : 2 * hi].bitcast(FP4X4),
                 rhs_scale=x_plane[:, lo:hi],
                 start=True,
@@ -156,81 +146,79 @@ def tile_list_head_blend_two_lists_pl_kernel(
             else:
                 nc.scalar.copy(out=z[t][:, lo:hi], in_=acc[:])
 
-        gates(0, 0, 2, 4)
+        gates(0, 0, 1, 4)
         features(0, 0, 256, 0, True)
         features(0, 256, 512, 7, True)
         features(1, 0, 512, 1, False)
-        gates(0, 2, 4, 0)
+        gates(0, 1, 2, 0)
         features(2, 0, 512, 7, False)
-        features(3, 0, 512, 1, False)
+        gates(0, 2, 4, 1)
+        features(3, 0, 512, 0, False)
 
         y_codes = keep.tile([P, W], I32, name="y_codes", align_bytes=64)
         y_plane = keep.tile([P, W], U8, name="y_plane", align_bytes=64)
         out_rows = out_0.rearrange("(p t) j -> p t j", t=PACK)
         out_words = out_1[0].rearrange("p n t -> p (n t)")
-        part_a = [keep.tile([P, PACK, n], F32, name="part_a%d" % c) for c, (j0, n) in enumerate(CHUNKS)]
-        part_b = [keep.tile([P, PACK, n], F32, name="part_b%d" % c) for c, (j0, n) in enumerate(CHUNKS)]
-        y_bf = [keep.tile([P, PACK * n], BF16, name="y_bf%d" % c, align_bytes=64) for c, (j0, n) in enumerate(CHUNKS)]
+        part_a = [keep.tile([P, PACK, HALF], F32, name="part_a%d" % h) for h in range(2)]
+        part_b = [keep.tile([P, PACK, HALF], F32, name="part_b%d" % h) for h in range(2)]
+        y_bf = keep.tile([P, PACK * W], BF16, name="y_bf", align_bytes=64)
         y = {}
 
-        def look_up(c, t):
-            j0, n = CHUNKS[c]
-            cols = slice(j0 // 16, (j0 + n) // 16)
-            nc.vector.tensor_tensor(part_a[c][:, t, :], z[t][:].indirect(list_a[:, cols]), gate_a[c][:, t, :], MULT)
-            nc.vector.tensor_tensor(part_b[c][:, t, :], z[t][:].indirect(list_b[:, cols]), gate_b[c][:, t, :], MULT)
+        def look_up(parts, offsets, gate, h, t, lo, hi):
+            cols = slice((h * HALF + lo) // 16, (h * HALF + hi) // 16)
+            nc.vector.tensor_tensor(parts[h][:, t, lo:hi], z[t][:].indirect(offsets[:, cols]), gate[h][:, t, lo:hi], MULT)
 
-        def add(c, t0, t1):
-            nc.vector.tensor_tensor(y[c][:, t0:t1, :], part_a[c][:, t0:t1, :], part_b[c][:, t0:t1, :], ADD)
+        def look_up_both(h, t, lo, hi):
+            look_up(part_a, list_a, gate_a, h, t, lo, hi)
+            look_up(part_b, list_b, gate_b, h, t, lo, hi)
 
-        def store(c):
-            j0, n = CHUNKS[c]
-            nc.sync.dma_start(out=out_rows[:, :, j0 : j0 + n], in_=y[c][:])
+        def add(h, t0, t1, lo, hi):
+            nc.vector.tensor_tensor(y[h][:, t0:t1, lo:hi], part_a[h][:, t0:t1, lo:hi], part_b[h][:, t0:t1, lo:hi], ADD)
 
-        def round_y(c, on_vector):
-            dst, src = interleave_views(y_bf[c][:], y[c][:])
-            if on_vector:
-                nc.vector.tensor_copy(out=dst, in_=src)
-            else:
-                nc.scalar.copy(out=dst, in_=src)
+        def store(h, t0, t1, lo, hi):
+            nc.sync.dma_start(out=out_rows[:, t0:t1, h * HALF + lo : h * HALF + hi], in_=y[h][:, t0:t1, lo:hi])
 
-        def planes(c):
-            j0, n = CHUNKS[c]
+        def round_y(h, lo, hi, on_vector):
+            round_rows(y_bf[:, PACK * (h * HALF + lo) : PACK * (h * HALF + hi)], y[h][:, :, lo:hi], on_vector)
+
+        def planes(j0, j1):
             nc.vector.quantize_mx(
-                out=y_codes[:, j0 : j0 + n].bitcast(FP8X4), scales=y_plane[:, j0 : j0 + n], in_=y_bf[c][:]
+                out=y_codes[:, j0:j1].bitcast(FP8X4), scales=y_plane[:, j0:j1], in_=y_bf[:, PACK * j0 : PACK * j1]
             )
-            nc.sync.dma_start(out=out_words[:, 4 * j0 : 4 * (j0 + n)].bitcast(I32), in_=y_codes[:, j0 : j0 + n])
 
-        round_q(1, False)
-        round_q(2, False)
+        def store_words(j0, j1):
+            nc.sync.dma_start(out=out_words[:, 4 * j0 : 4 * j1].bitcast(I32), in_=y_codes[:, j0:j1])
+
+        round_rows(q_bf[1][:], q_rows[1][:], False)
         for t in range(PACK):
-            look_up(0, t)
+            look_up_both(0, t, 0, HALF)
         quantise_q(1)
-        gates(1, 0, 4, 5)
-        y[0] = keep.tile([P, PACK, CHUNKS[0][1]], F32, name="y0", tag="stage1", align_bytes=64)
-        add(0, 0, 4)
-        store(0)
-        quantise_q(2)
-        gates(2, 0, 4, 6)
-        round_y(0, False)
-        for t in range(PACK):
-            look_up(1, t)
-        y[1] = keep.tile([P, PACK, CHUNKS[1][1]], F32, name="y1", tag="stage2", align_bytes=64)
-        look_up(2, 0)
-        add(1, 0, 4)
-        store(1)
-        round_y(1, False)
-        y[2] = keep.tile([P, PACK, CHUNKS[2][1]], F32, name="y2")
-        look_up(2, 1)
-        look_up(2, 2)
-        add(2, 0, 2)
-        look_up(2, 3)
-        add(2, 2, 3)
-        planes(0)
-        add(2, 3, 4)
-        store(2)
-        planes(1)
-        round_y(2, True)
-        planes(2)
+        gates(1, 0, 2, 5)
+        gates(1, 2, 4, 6)
+        y[0] = keep.tile([P, PACK, HALF], F32, name="y0", tag="stage1", align_bytes=64)
+        add(0, 0, 4, 0, HALF)
+        store(0, 0, 4, 0, HALF)
+        round_y(0, 0, HALF, False)
+        y[1] = keep.tile([P, PACK, HALF], F32, name="y1")
+        look_up_both(1, 0, 0, HALF)
+        look_up_both(1, 1, 0, HALF)
+        look_up_both(1, 2, 0, HALF)
+        planes(0, HALF)
+        store_words(0, HALF)
+        look_up(part_a, list_a, gate_a, 1, 3, 0, 128)
+        add(1, 0, 3, 0, HALF)
+        store(1, 0, 3, 0, HALF)
+        look_up(part_b, list_b, gate_b, 1, 3, 0, 128)
+        look_up(part_a, list_a, gate_a, 1, 3, 128, 256)
+        add(1, 3, 4, 0, 128)
+        round_y(1, 0, 128, False)
+        look_up(part_b, list_b, gate_b, 1, 3, 128, 256)
+        add(1, 3, 4, 128, 256)
+        store(1, 3, 4, 0, HALF)
+        round_y(1, 128, 256, True)
+        planes(256, 384)
+        planes(384, 512)
+        store_words(HALF, W)
         for q in range(4):
             queue = nc.scalar if q % 2 else nc.sync
             queue.dma_start(

@@ -121,8 +121,7 @@ def tile_list_head_blend_two_lists_pl_kernel(
             nc.scalar.activation(out=gate_a[h][:, t0:t1, :], in_=g[:], func=SIGMOID)
             nc.scalar.activation(out=gate_b[h][:, t0:t1, :], in_=g[:], func=SIGMOID, scale=-1.0)
 
-        round_rows(q_bf[0][:, : PACK * 160], q_rows[0][:, :, :160], True)
-        round_rows(q_bf[0][:, PACK * 160 :], q_rows[0][:, :, 160:], False)
+        round_rows(q_bf[0][:], q_rows[0][:], True)
         quantise_q(0)
         deal_scales(nc, planes_dealt, planes_raw)
         w_codes = keep.tile([P, W], I32, name="w_codes", tag="stage0", align_bytes=64)
@@ -146,14 +145,13 @@ def tile_list_head_blend_two_lists_pl_kernel(
             else:
                 nc.scalar.copy(out=z[t][:, lo:hi], in_=acc[:])
 
-        gates(0, 0, 1, 4)
+        gates(0, 0, 2, 4)
         features(0, 0, 256, 0, True)
         features(0, 256, 512, 7, True)
         features(1, 0, 512, 1, False)
-        gates(0, 1, 2, 0)
+        gates(0, 2, 4, 0)
         features(2, 0, 512, 7, False)
-        gates(0, 2, 4, 1)
-        features(3, 0, 512, 0, False)
+        features(3, 0, 512, 1, False)
 
         y_codes = keep.tile([P, W], I32, name="y_codes", align_bytes=64)
         y_plane = keep.tile([P, W], U8, name="y_plane", align_bytes=64)
@@ -193,7 +191,8 @@ def tile_list_head_blend_two_lists_pl_kernel(
         for t in range(PACK):
             look_up_both(0, t, 0, HALF)
         quantise_q(1)
-        gates(1, 0, 2, 5)
+        gates(1, 0, 1, 5)
+        gates(1, 1, 2, 2)
         gates(1, 2, 4, 6)
         y[0] = keep.tile([P, PACK, HALF], F32, name="y0", tag="stage1", align_bytes=64)
         add(0, 0, 4, 0, HALF)

@@ -1,6 +1,7 @@
 from contextlib import ExitStack
 
 import concourse.mybir as mybir
+from concourse.masks import make_identity
 
 F32 = mybir.dt.float32
 BF16 = mybir.dt.bfloat16
@@ -66,7 +67,9 @@ def tile_list_head_blend_two_lists_pl_kernel(
         x_codes = keep.tile([P, 2 * W], U8, name="x_codes", align_bytes=64)
         planes_raw = keep.tile([P, W], U8, name="planes_raw")
         x_plane = keep.tile([P, W], U8, name="x_plane", align_bytes=64)
-        q_rows = [keep.tile([P, PACK, HALF], F32, name="q_rows%d" % h) for h in range(2)]
+        q_rows = [keep.tile([P, PACK, HALF], F32, name="q_rows%d" % h, tag="q_rows%d" % h) for h in range(2)]
+        identity = keep.tile([P, P], F32, name="identity")
+        make_identity(nc, identity[:])
 
         nc.vector.memset(planes_raw[:].bitcast(I32), 0)
         nc.vector.memset(x_plane[:].bitcast(I32), 0)
@@ -127,7 +130,7 @@ def tile_list_head_blend_two_lists_pl_kernel(
         w_codes = keep.tile([P, W], I32, name="w_codes", tag="stage0", align_bytes=64)
         deal_words(nc, w_codes, w_raw)
 
-        z = [keep.tile([P, W], F32, name="z%d" % t) for t in range(PACK)]
+        z = [keep.tile([P, W], F32, name="z%d" % t) for t in range(PACK - 1)]
 
         def features(t, lo, hi, bank, on_vector):
             acc = psum.tile([P, hi - lo], F32, name="z_acc%d_%d" % (t, lo), tag="bank%d" % bank)
@@ -151,6 +154,8 @@ def tile_list_head_blend_two_lists_pl_kernel(
         features(1, 0, 512, 1, False)
         gates(0, 2, 4, 0)
         features(2, 0, 512, 7, False)
+        round_rows(q_bf[1][:], q_rows[1][:], False)
+        z.append(keep.tile([P, W], F32, name="z3", tag="q_rows1"))
         features(3, 0, 512, 1, False)
 
         y_codes = keep.tile([P, W], I32, name="y_codes", align_bytes=64)
@@ -159,7 +164,8 @@ def tile_list_head_blend_two_lists_pl_kernel(
         out_words = out_1[0].rearrange("p n t -> p (n t)")
         part_a = [keep.tile([P, PACK, HALF], F32, name="part_a%d" % h) for h in range(2)]
         part_b = [keep.tile([P, PACK, HALF], F32, name="part_b%d" % h) for h in range(2)]
-        y_bf = keep.tile([P, PACK * W], BF16, name="y_bf", align_bytes=64)
+        y_first = keep.tile([P, 2, PACK * P], BF16, name="y_first", align_bytes=64)
+        y_bf = [y_first[:, 0, :], y_first[:, 1, :]]
         y = {}
 
         def look_up(parts, offsets, gate, h, t, lo, hi):
@@ -176,47 +182,58 @@ def tile_list_head_blend_two_lists_pl_kernel(
         def store(h, t0, t1, lo, hi):
             nc.sync.dma_start(out=out_rows[:, t0:t1, h * HALF + lo : h * HALF + hi], in_=y[h][:, t0:t1, lo:hi])
 
-        def round_y(h, lo, hi, on_vector):
-            round_rows(y_bf[:, PACK * (h * HALF + lo) : PACK * (h * HALF + hi)], y[h][:, :, lo:hi], on_vector)
-
-        def planes(j0, j1):
-            nc.vector.quantize_mx(
-                out=y_codes[:, j0:j1].bitcast(FP8X4), scales=y_plane[:, j0:j1], in_=y_bf[:, PACK * j0 : PACK * j1]
-            )
+        def planes(j0, j1, rounded):
+            nc.vector.quantize_mx(out=y_codes[:, j0:j1].bitcast(FP8X4), scales=y_plane[:, j0:j1], in_=rounded)
 
         def store_words(j0, j1):
             nc.sync.dma_start(out=out_words[:, 4 * j0 : 4 * j1].bitcast(I32), in_=y_codes[:, j0:j1])
 
-        round_rows(q_bf[1][:], q_rows[1][:], False)
-        for t in range(PACK):
+        for t in range(PACK - 1):
             look_up_both(0, t, 0, HALF)
         quantise_q(1)
+        look_up_both(0, 3, 0, HALF)
         gates(1, 0, 1, 5)
         gates(1, 1, 2, 2)
         gates(1, 2, 4, 6)
-        y[0] = keep.tile([P, PACK, HALF], F32, name="y0", tag="stage1", align_bytes=64)
-        add(0, 0, 4, 0, HALF)
-        store(0, 0, 4, 0, HALF)
-        round_y(0, 0, HALF, False)
+
+        y[0] = keep.tile([P, PACK, HALF], F32, name="y0")
+        turned = keep.tile([P, 2, PACK, P], F32, name="turned", tag="turned", align_bytes=64)
+        for b, bank in enumerate((5, 2)):
+            cols = slice(b * P, (b + 1) * P)
+            summed = psum.tile([P, PACK, P], F32, name="summed%d" % b, tag="bank%d" % bank)
+            for t in range(PACK):
+                nc.tensor.matmul(summed[:, t, :], part_a[0][:, t, cols], identity[:], start=True, stop=False, is_transpose=True)
+                nc.tensor.matmul(summed[:, t, :], part_b[0][:, t, cols], identity[:], start=False, stop=True, is_transpose=True)
+            nc.scalar.copy(out=turned[:, b, :, :], in_=summed[:])
+        for b, bank in enumerate((3, 4)):
+            cols = slice(b * P, (b + 1) * P)
+            back = psum.tile([P, PACK, P], F32, name="back%d" % b, tag="bank%d" % bank)
+            for t in range(PACK):
+                nc.tensor.transpose(back[:, t, :], turned[:, b, t, :], identity[:])
+            nc.scalar.copy(out=y[0][:, :, cols], in_=back[:])
+            nc.scalar.dma_start(out=out_rows[:, :, cols], in_=y[0][:, :, cols])
+            round_rows(y_bf[b], back[:], False)
+        y_bf.append(keep.tile([P, PACK * P], BF16, name="y_bf2", tag="turned", align_bytes=64))
+        y_bf.append(keep.tile([P, PACK * P], BF16, name="y_bf3", align_bytes=64))
         y[1] = keep.tile([P, PACK, HALF], F32, name="y1")
         look_up_both(1, 0, 0, HALF)
         look_up_both(1, 1, 0, HALF)
         look_up_both(1, 2, 0, HALF)
-        planes(0, HALF)
-        store_words(0, HALF)
         look_up(part_a, list_a, gate_a, 1, 3, 0, 128)
         add(1, 0, 3, 0, HALF)
         store(1, 0, 3, 0, HALF)
         look_up(part_b, list_b, gate_b, 1, 3, 0, 128)
         look_up(part_a, list_a, gate_a, 1, 3, 128, 256)
         add(1, 3, 4, 0, 128)
-        round_y(1, 0, 128, False)
+        round_rows(y_bf[2][:], y[1][:, :, 0:128], False)
         look_up(part_b, list_b, gate_b, 1, 3, 128, 256)
         add(1, 3, 4, 128, 256)
         store(1, 3, 4, 0, HALF)
-        round_y(1, 128, 256, True)
-        planes(256, 384)
-        planes(384, 512)
+        planes(0, HALF, y_first[:].rearrange("p b c -> p (b c)"))
+        store_words(0, HALF)
+        round_rows(y_bf[3][:], y[1][:, :, 128:256], True)
+        planes(256, 384, y_bf[2][:])
+        planes(384, 512, y_bf[3][:])
         store_words(HALF, W)
         for q in range(4):
             queue = nc.scalar if q % 2 else nc.sync

from contextlib import ExitStack

import concourse.mybir as mybir
from concourse.masks import make_identity

F32 = mybir.dt.float32
BF16 = mybir.dt.bfloat16
I32 = mybir.dt.int32
U16 = mybir.dt.uint16
U8 = mybir.dt.uint8
FP8X4 = mybir.dt.float8_e4m3fn_x4
FP4X4 = mybir.dt.float4_e2m1fn_x4
MULT = mybir.AluOpType.mult
ADD = mybir.AluOpType.add
SIGMOID = mybir.ActivationFunctionType.Sigmoid

P = 128
PACK = 4
W = 512
BANK = 512
FLOPS = 2 * 2 * 512 * 512 * 512

HALF = 256


def load_scales(queue, plane, first_row, scales, quadrants):
    for q in quadrants:
        queue.dma_start(
            out=plane[32 * q + first_row : 32 * q + first_row + 4, :].bitcast(I32),
            in_=scales[0, 4 * q : 4 * q + 4, :].bitcast(I32),
        )


def deal_words(nc, dealt, raw):
    nc.vector.tensor_copy(
        out=dealt[:].rearrange("p (t c i) -> p c t i", t=PACK, i=4),
        in_=raw[:].rearrange("p (c i t) -> p c t i", t=PACK, i=4),
    )


def deal_scales(nc, dealt, raw):
    nc.vector.tensor_copy(
        out=dealt[:].rearrange("p (t c i) -> p c t i", t=PACK, i=16),
        in_=raw[:].rearrange("p (c i t) -> p c t i", t=PACK, i=16),
    )


def interleave_views(grouped, rows):
    return (
        grouped.rearrange("p (c i t) -> p c t i", t=PACK, i=4),
        rows.rearrange("p t (c i) -> p c t i", i=4),
    )


def tile_list_head_blend_two_lists_pl_kernel(
    tc, xt_words, xt_scales, w_words, w_scales, qx, wq_words, wq_scales, offs, offs2, out_0, out_1, out_2
):
    nc = tc.nc
    with ExitStack() as ctx:
        keep = ctx.enter_context(tc.tile_pool(name="keep", bufs=1))
        psum = ctx.enter_context(tc.psum_pool(name="psum", bufs=1))

        list_a = keep.tile([P, W // 16], U16, name="list_a")
        list_b = keep.tile([P, W // 16], U16, name="list_b")
        wq_raw = keep.tile([P, W], I32, name="wq_raw")
        w_raw = keep.tile([P, W], I32, name="w_raw")
        x_codes = keep.tile([P, 2 * W], U8, name="x_codes", align_bytes=64)
        planes_raw = keep.tile([P, W], U8, name="planes_raw")
        x_plane = keep.tile([P, W], U8, name="x_plane", align_bytes=64)
        q_rows = [keep.tile([P, PACK, HALF], F32, name="q_rows%d" % h, tag="q_rows%d" % h) for h in range(2)]
        identity = keep.tile([P, P], F32, name="identity")
        make_identity(nc, identity[:])

        nc.vector.memset(planes_raw[:].bitcast(I32), 0)
        nc.vector.memset(x_plane[:].bitcast(I32), 0)

        qx_rows = qx.rearrange("(p r) j -> p r j", r=PACK)
        nc.sync.dma_start(out=wq_raw[:], in_=wq_words[0].rearrange("p n t -> p (n t)").bitcast(I32))
        load_scales(nc.scalar, planes_raw, 4, wq_scales, (0, 1, 2))
        load_scales(nc.sync, planes_raw, 4, wq_scales, (3,))
        load_scales(nc.sync, planes_raw, 0, w_scales, (0, 1))
        nc.sync.dma_start(out=q_rows[0][:], in_=qx_rows[:, :, 0:HALF])
        load_scales(nc.sync, planes_raw, 0, w_scales, (2, 3))
        nc.sync.dma_start(out=w_raw[:], in_=w_words[0].rearrange("p n t -> p (n t)").bitcast(I32))
        nc.sync.dma_start(out=x_codes[:].bitcast(I32), in_=xt_words[0].bitcast(I32))
        load_scales(nc.sync, x_plane, 0, xt_scales, (0, 1, 2, 3))
        nc.sync.dma_start(list_a[:], offs)
        nc.sync.dma_start(list_b[:], offs2)
        nc.sync.dma_start(out=q_rows[1][:], in_=qx_rows[:, :, HALF:W])

        wq_codes = keep.tile([P, W], I32, name="wq_codes", align_bytes=64)
        planes_dealt = keep.tile([P, W], U8, name="planes_dealt", align_bytes=64)
        deal_words(nc, wq_codes, wq_raw)

        q_codes = [keep.tile([P, HALF], I32, name="q_codes%d" % h, align_bytes=64) for h in range(2)]
        q_plane = [keep.tile([P, HALF], U8, name="q_plane%d" % h, align_bytes=64) for h in range(2)]
        q_bf = [keep.tile([P, PACK * HALF], BF16, name="q_bf%d" % h, tag="stage%d" % h, align_bytes=64) for h in range(2)]

        def round_rows(grouped, rows, on_vector):
            dst, src = interleave_views(grouped, rows)
            if on_vector:
                nc.vector.tensor_copy(out=dst, in_=src)
            else:
                nc.scalar.copy(out=dst, in_=src)

        def quantise_q(h):
            nc.vector.quantize_mx(out=q_codes[h][:].bitcast(FP8X4), scales=q_plane[h][:], in_=q_bf[h][:])

        gate_a = [keep.tile([P, PACK, HALF], F32, name="gate_a%d" % h) for h in range(2)]
        gate_b = [keep.tile([P, PACK, HALF], F32, name="gate_b%d" % h) for h in range(2)]

        def gates(h, t0, t1, bank):
            g = psum.tile([P, t1 - t0, HALF], F32, name="g%d_%d" % (h, t0), tag="bank%d" % bank)
            for t in range(t0, t1):
                nc.tensor.matmul_mx(
                    out=g[:, t - t0, :],
                    lhsT=wq_codes[:, t * P : (t + 1) * P].bitcast(FP8X4),
                    lhsT_scale=planes_dealt[4:P, t * P : (t + 1) * P],
                    rhs=q_codes[h][:].bitcast(FP8X4),
                    rhs_scale=q_plane[h][:],
                    start=True,
                    stop=True,
                )
            nc.scalar.activation(out=gate_a[h][:, t0:t1, :], in_=g[:], func=SIGMOID)
            nc.scalar.activation(out=gate_b[h][:, t0:t1, :], in_=g[:], func=SIGMOID, scale=-1.0)

        round_rows(q_bf[0][:], q_rows[0][:], True)
        quantise_q(0)
        deal_scales(nc, planes_dealt, planes_raw)
        w_codes = keep.tile([P, W], I32, name="w_codes", tag="stage0", align_bytes=64)
        deal_words(nc, w_codes, w_raw)

        z = [keep.tile([P, W], F32, name="z%d" % t) for t in range(PACK - 1)]

        def features(t, lo, hi, bank, on_vector):
            acc = psum.tile([P, hi - lo], F32, name="z_acc%d_%d" % (t, lo), tag="bank%d" % bank)
            nc.tensor.matmul_mx(
                out=acc[:],
                lhsT=w_codes[:, t * P : (t + 1) * P].bitcast(FP8X4),
                lhsT_scale=planes_dealt[:, t * P : (t + 1) * P],
                rhs=x_codes[:, 2 * lo : 2 * hi].bitcast(FP4X4),
                rhs_scale=x_plane[:, lo:hi],
                start=True,
                stop=True,
            )
            if on_vector:
                nc.vector.tensor_copy(out=z[t][:, lo:hi], in_=acc[:])
            else:
                nc.scalar.copy(out=z[t][:, lo:hi], in_=acc[:])

        gates(0, 0, 2, 4)
        features(0, 0, 256, 0, True)
        features(0, 256, 512, 7, True)
        features(1, 0, 512, 1, False)
        gates(0, 2, 4, 0)
        features(2, 0, 512, 7, False)
        round_rows(q_bf[1][:], q_rows[1][:], False)
        z.append(keep.tile([P, W], F32, name="z3", tag="q_rows1"))
        features(3, 0, 512, 1, False)

        y_codes = keep.tile([P, W], I32, name="y_codes", align_bytes=64)
        y_plane = keep.tile([P, W], U8, name="y_plane", align_bytes=64)
        out_rows = out_0.rearrange("(p t) j -> p t j", t=PACK)
        out_words = out_1[0].rearrange("p n t -> p (n t)")
        part_a = [keep.tile([P, PACK, HALF], F32, name="part_a%d" % h) for h in range(2)]
        part_b = [keep.tile([P, PACK, HALF], F32, name="part_b%d" % h) for h in range(2)]
        y_first = keep.tile([P, 2, PACK * P], BF16, name="y_first", align_bytes=64)
        y_bf = [y_first[:, 0, :], y_first[:, 1, :]]
        y = {}

        def look_up(parts, offsets, gate, h, t, lo, hi):
            cols = slice((h * HALF + lo) // 16, (h * HALF + hi) // 16)
            nc.vector.tensor_tensor(parts[h][:, t, lo:hi], z[t][:].indirect(offsets[:, cols]), gate[h][:, t, lo:hi], MULT)

        def look_up_both(h, t, lo, hi):
            look_up(part_a, list_a, gate_a, h, t, lo, hi)
            look_up(part_b, list_b, gate_b, h, t, lo, hi)

        def add(h, t0, t1, lo, hi):
            nc.vector.tensor_tensor(y[h][:, t0:t1, lo:hi], part_a[h][:, t0:t1, lo:hi], part_b[h][:, t0:t1, lo:hi], ADD)

        def store(h, t0, t1, lo, hi):
            nc.sync.dma_start(out=out_rows[:, t0:t1, h * HALF + lo : h * HALF + hi], in_=y[h][:, t0:t1, lo:hi])

        def planes(j0, j1, rounded):
            nc.vector.quantize_mx(out=y_codes[:, j0:j1].bitcast(FP8X4), scales=y_plane[:, j0:j1], in_=rounded)

        def store_words(j0, j1):
            nc.sync.dma_start(out=out_words[:, 4 * j0 : 4 * j1].bitcast(I32), in_=y_codes[:, j0:j1])

        for t in range(PACK - 1):
            look_up_both(0, t, 0, HALF)
        quantise_q(1)
        look_up_both(0, 3, 0, HALF)
        gates(1, 0, 1, 5)
        gates(1, 1, 2, 2)
        gates(1, 2, 4, 6)

        y[0] = keep.tile([P, PACK, HALF], F32, name="y0")
        turned = keep.tile([P, 2, PACK, P], F32, name="turned", tag="turned", align_bytes=64)
        for b, bank in enumerate((5, 2)):
            cols = slice(b * P, (b + 1) * P)
            summed = psum.tile([P, PACK, P], F32, name="summed%d" % b, tag="bank%d" % bank)
            for t in range(PACK):
                nc.tensor.matmul(summed[:, t, :], part_a[0][:, t, cols], identity[:], start=True, stop=False, is_transpose=True)
                nc.tensor.matmul(summed[:, t, :], part_b[0][:, t, cols], identity[:], start=False, stop=True, is_transpose=True)
            nc.scalar.copy(out=turned[:, b, :, :], in_=summed[:])
        for b, bank in enumerate((3, 4)):
            cols = slice(b * P, (b + 1) * P)
            back = psum.tile([P, PACK, P], F32, name="back%d" % b, tag="bank%d" % bank)
            for t in range(PACK):
                nc.tensor.transpose(back[:, t, :], turned[:, b, t, :], identity[:])
            nc.scalar.copy(out=y[0][:, :, cols], in_=back[:])
            nc.scalar.dma_start(out=out_rows[:, :, cols], in_=y[0][:, :, cols])
            round_rows(y_bf[b], back[:], False)
        y_bf.append(keep.tile([P, PACK * P], BF16, name="y_bf2", tag="turned", align_bytes=64))
        y_bf.append(keep.tile([P, PACK * P], BF16, name="y_bf3", align_bytes=64))
        y[1] = keep.tile([P, PACK, HALF], F32, name="y1")
        look_up_both(1, 0, 0, HALF)
        look_up_both(1, 1, 0, HALF)
        look_up_both(1, 2, 0, HALF)
        look_up(part_a, list_a, gate_a, 1, 3, 0, 128)
        add(1, 0, 3, 0, HALF)
        store(1, 0, 3, 0, HALF)
        look_up(part_b, list_b, gate_b, 1, 3, 0, 128)
        look_up(part_a, list_a, gate_a, 1, 3, 128, 256)
        add(1, 3, 4, 0, 128)
        round_rows(y_bf[2][:], y[1][:, :, 0:128], False)
        look_up(part_b, list_b, gate_b, 1, 3, 128, 256)
        add(1, 3, 4, 128, 256)
        store(1, 3, 4, 0, HALF)
        planes(0, HALF, y_first[:].rearrange("p b c -> p (b c)"))
        store_words(0, HALF)
        round_rows(y_bf[3][:], y[1][:, :, 128:256], True)
        planes(256, 384, y_bf[2][:])
        planes(384, 512, y_bf[3][:])
        store_words(HALF, W)
        for q in range(4):
            queue = nc.scalar if q % 2 else nc.sync
            queue.dma_start(
                out=out_2[0, 4 * q : 4 * q + 4, :].bitcast(I32),
                in_=y_plane[32 * q : 32 * q + 4, :].bitcast(I32),
            )
